import numpy as np
import ml_dtypes


def mxq(x, axis, fmt="e4m3"):
    dtype, down = {"e4m3": (ml_dtypes.float8_e4m3fn, 7), "e5m2": (ml_dtypes.float8_e5m2, 14)}[fmt]
    v = np.moveaxis(np.asarray(x, np.float32).astype(ml_dtypes.bfloat16).astype(np.float64), axis, -1)
    blocks = v.reshape(v.shape[:-1] + (-1, 32))
    amax = np.abs(blocks).max(-1, keepdims=True)
    byte = np.maximum(np.where(amax > 0, np.frexp(amax)[1] - 1 + 127, 0) - down, 1)
    scale = np.exp2(byte - 127.0)
    codes = (blocks / scale).astype(np.float32).astype(dtype).astype(np.float64)
    return np.moveaxis((codes * scale).reshape(v.shape), -1, axis)


WIDE = False


def mx_kscale(k):
    if not WIDE:
        return np.ones(k)
    levels = np.array([30, -30])
    if k % 512:
        return np.exp2(np.random.permutation(np.resize(levels, k // 32))).repeat(32)
    a = np.empty((k // 512, 16))
    for p in range(k // 512):
        a[p, :8] = np.random.permutation(np.resize(levels, 8))
        for g in range(8):
            far = levels[np.abs(levels - a[p, g]) >= 10]
            a[p, g + 8] = far[np.random.randint(len(far))]
    return np.exp2(a.ravel()).repeat(32)


def f64(x):
    return np.asarray(x).astype(np.float64)


def striped(idx):
    return np.tile(np.asarray(idx).reshape(-1, 16).T, (8, 1)).astype(np.uint16)


def unstriped(offs):
    return offs[:16].T.reshape(-1).astype(np.int64)


E2M1 = np.array([0.0, 0.5, 1.0, 1.5, 2.0, 3.0, 4.0, 6.0, -0.0, -0.5, -1.0, -1.5, -2.0, -3.0, -4.0, -6.0])


def pack_weight(w, fmt):
    k, n = w.shape
    w = f64(np.asarray(w, np.float32).astype(ml_dtypes.bfloat16)).reshape(k // 32, 32, n)
    amax = np.abs(w).max(1)
    if fmt in ("e4m3", "e5m2"):
        byte = np.frexp(amax)[1] - 1 + 127 - (7 if fmt == "e4m3" else 14)
    else:
        mant, ex = np.frexp(amax / 6.0)
        byte = np.where(mant > 0.5, ex, ex - 1) + 127
    byte = np.clip(np.where(amax > 0, byte, 1), 1, 254)
    scaled = (w * np.exp2(127.0 - byte)[:, None, :]).reshape(k, n).astype(np.float32)
    by_word = np.ascontiguousarray(scaled.reshape(k // 512, 128, 4, n).transpose(0, 1, 3, 2))
    if fmt in ("e4m3", "e5m2"):
        words = by_word.astype(ml_dtypes.float8_e4m3fn if fmt == "e4m3" else ml_dtypes.float8_e5m2).view(np.uint8)
    else:
        c = by_word.astype(ml_dtypes.float4_e2m1fn).view(np.uint8) & 0xF
        words = (c[..., 0::2] | (c[..., 1::2] << 4)).reshape(k // 512, 128, 2 * n)
    return np.ascontiguousarray(words), np.ascontiguousarray(byte.astype(np.uint8).reshape(k // 512, 16, n))


def unpack_weight(words, scales, fmt):
    g, _, n = scales.shape
    words = np.ascontiguousarray(words).reshape(g, 128, n, -1)
    if fmt in ("e4m3", "e5m2"):
        vals = words.view(ml_dtypes.float8_e4m3fn if fmt == "e4m3" else ml_dtypes.float8_e5m2).astype(np.float64)
    else:
        nib = np.empty((g, 128, n, 4), np.uint8)
        nib[..., 0::2] = words & 0xF
        nib[..., 1::2] = words >> 4
        vals = E2M1[nib]
    vals = vals * np.repeat(np.exp2(scales.astype(np.float64) - 127.0), 8, axis=1)[..., None]
    return vals.transpose(0, 1, 3, 2).reshape(g * 512, n)


def bf(x):
    return np.asarray(x, np.float32).astype(ml_dtypes.bfloat16)


def planes(Y):
    r, m = Y.shape
    b = f64(bf(Y)).reshape(r // 32, 32, m)
    amax = np.abs(b).max(1)
    byte = np.clip(np.where(amax > 0, np.frexp(amax)[1] - 1 + 127 - 7, 1), 1, 254)
    codes = (b * np.exp2(127.0 - byte)[:, None, :]).reshape(r, m).astype(np.float32).astype(ml_dtypes.float8_e4m3fn).view(np.uint8)
    words = codes.reshape(r // 512, 128, 4, m).transpose(0, 1, 3, 2)
    return np.ascontiguousarray(words), np.ascontiguousarray(byte.astype(np.uint8).reshape(r // 512, 16, m))


K, T, J, R, O, N, Z = 512, 512, 256, 512, 128, 512, 512


def setup_inputs():
    n = np.random.standard_normal
    idx = np.random.permutation(T)[:J]
    idx2 = np.random.permutation(J)[:O]
    idx3 = np.random.permutation(J)[:O]
    idx4 = np.random.permutation(Z)[:O]
    fk = mx_kscale(K)
    fr = mx_kscale(R)
    xtp = pack_weight(n((K, T)) / fk[:, None], "e4m3")
    wp = pack_weight(n((K, R)) * 1 / np.sqrt(K) * fk[:, None] * fr, "e5m2")
    wbp = pack_weight(n((R, N)) * 1 / np.sqrt(R) / fr[:, None], "e2m1")
    return {
        "xt_words": xtp[0],
        "xt_scales": xtp[1],
        "w_words": wp[0],
        "w_scales": wp[1],
        "wb_words": wbp[0],
        "wb_scales": wbp[1],
        "tz": (n((N, Z)) * 0.6).astype(np.float32),
        "rw": (np.random.uniform(0.5, 2.0, (1, O))).astype(np.float32),
        "offs": striped(idx),
        "offs2": striped(idx2),
        "offs3": striped(idx3),
        "offs4": striped(idx4),
    }


def reference(xt_words, xt_scales, w_words, w_scales, wb_words, wb_scales, tz, rw, offs, offs2, offs3, offs4):
    idx = unstriped(offs)
    idx2 = unstriped(offs2)
    idx3 = unstriped(offs3)
    idx4 = unstriped(offs4)
    xtu = unpack_weight(xt_words, xt_scales, "e4m3")
    wu = unpack_weight(w_words, w_scales, "e5m2")
    wbu = unpack_weight(wb_words, wb_scales, "e2m1")
    xtidxg = xtu[:, idx]
    a = wu.T @ xtidxg
    hid = np.maximum(a[:, idx2], a[:, idx3])
    hidq = mxq(hid, 0, "e5m2")
    p = wbu.T @ hidq
    y = np.maximum(p, f64(tz)[:, idx4]) * f64(rw)
    words, scales = planes(y)
    return y, words, scales

@@ -1,0 +1,197 @@
+from contextlib import ExitStack
+
+import concourse.mybir as mybir
+
+K, T, J, R, O, N, Z = 512, 512, 256, 512, 128, 512, 512
+FLOPS = 2 * K * R * J + 2 * R * N * O
+
+F32 = mybir.dt.float32
+BF16 = mybir.dt.bfloat16
+I32 = mybir.dt.int32
+U32 = mybir.dt.uint32
+U16 = mybir.dt.uint16
+U8 = mybir.dt.uint8
+E4M3 = mybir.dt.float8_e4m3fn_x4
+E5M2 = mybir.dt.float8_e5m2_x4
+E2M1 = mybir.dt.float4_e2m1fn_x4
+COPY = mybir.ActivationFunctionType.Copy
+MAX = mybir.AluOpType.max
+MULT = mybir.AluOpType.mult
+
+P = 128
+PACK = 4
+QUADS = 4
+QUAD = P // QUADS
+
+
+def load_scales_quadrant(queue, plane, scales, q):
+    rows = scales[0, PACK * q : PACK * (q + 1), :].bitcast(I32)
+    queue.dma_start(
+        out=plane[QUAD * q : QUAD * (q + 1), :].bitcast(I32),
+        in_=rows.unsqueeze(0).to_broadcast([QUAD // PACK, PACK, rows.shape[1]]),
+    )
+
+
+def tile_list_looks_picked_larger_floored_pl_kernel(
+    tc, xt_words, xt_scales, w_words, w_scales, wb_words, wb_scales, tz, rw, offs, offs2, offs3, offs4, out_0, out_1, out_2
+):
+    nc = tc.nc
+    with ExitStack() as ctx:
+        sb = ctx.enter_context(tc.tile_pool(name="sb", bufs=1))
+        ps = ctx.enter_context(tc.psum_pool(name="ps", bufs=1))
+
+        list1 = sb.tile([P, J // 16], U16, name="list1")
+        list2 = sb.tile([P, O // 16], U16, name="list2")
+        list3 = sb.tile([P, O // 16], U16, name="list3")
+        list4 = sb.tile([P, O // 16], U16, name="list4")
+        x_words = sb.tile([P, T], U32, name="x_words", align_bytes=64)
+        x_plane = sb.tile([P, T], U8, name="x_plane", align_bytes=64)
+        w_raw = sb.tile([P, R], U32, name="w_raw", align_bytes=64)
+        w_plane_raw = sb.tile([P, R], U8, name="w_plane_raw", align_bytes=64)
+        wb_raw = sb.tile([P, N], U16, name="wb_raw", align_bytes=64)
+        wb_plane_raw = sb.tile([P, N], U8, name="wb_plane_raw", align_bytes=64)
+        tz_rows = [sb.tile([P, Z], F32, name="tz_rows%d" % t, align_bytes=64) for t in range(PACK)]
+        rw_all = sb.tile([P, O], F32, name="rw_all", align_bytes=64)
+
+        nc.sync.dma_start(list1[:], offs)
+        load_scales_quadrant(nc.scalar, x_plane, xt_scales, 0)
+        load_scales_quadrant(nc.sync, x_plane, xt_scales, 1)
+        load_scales_quadrant(nc.scalar, x_plane, xt_scales, 2)
+        load_scales_quadrant(nc.sync, x_plane, xt_scales, 3)
+        nc.scalar.dma_start(out=x_words[:].bitcast(I32), in_=xt_words[0].rearrange("p c t -> p (c t)").bitcast(I32))
+        load_scales_quadrant(nc.sync, w_plane_raw, w_scales, 0)
+        nc.scalar.dma_start(out=w_raw[:].bitcast(I32), in_=w_words[0].rearrange("p c t -> p (c t)").bitcast(I32))
+        for q in range(1, QUADS):
+            load_scales_quadrant(nc.sync, w_plane_raw, w_scales, q)
+        nc.sync.dma_start(list2[:], offs2)
+        nc.sync.dma_start(list3[:], offs3)
+        nc.sync.dma_start(out=wb_raw[:].bitcast(I32), in_=wb_words[0].bitcast(I32))
+        for q in range(QUADS):
+            load_scales_quadrant(nc.sync, wb_plane_raw, wb_scales, q)
+        nc.sync.dma_start(list4[:], offs4)
+        tz_dealt = tz.rearrange("(p t) z -> p t z", t=PACK)
+        for t in range(PACK):
+            nc.sync.dma_start(out=tz_rows[t][:], in_=tz_dealt[:, t, :])
+        nc.sync.dma_start(out=rw_all[:], in_=rw[0].partition_broadcast(P))
+
+        xg_words = sb.tile([P, J], U32, name="xg_words", align_bytes=64)
+        xg_plane = sb.tile([P, J], U8, name="xg_plane", align_bytes=64)
+        nc.vector.tensor_copy(xg_words[:], x_words[:].indirect(list1[:]))
+        nc.vector.tensor_copy(xg_plane[:], x_plane[:].indirect(list1[:]))
+
+        def deal(dealt, raw):
+            nc.vector.tensor_copy(
+                out=dealt.rearrange("p (t m) -> p m t", t=PACK), in_=raw.rearrange("p (m t) -> p m t", t=PACK)
+            )
+
+        w_dealt = sb.tile([P, R], U32, name="w_dealt", align_bytes=64)
+        w_plane = sb.tile([P, R], U8, name="w_plane", align_bytes=64)
+        deal(w_dealt[:].bitcast(I32), w_raw[:].bitcast(I32))
+
+        def deal_slot(dealt, raw, t):
+            nc.vector.tensor_copy(out=dealt[:, P * t : P * (t + 1)], in_=raw[:, t::PACK])
+
+        for t in range(PACK):
+            deal_slot(w_plane, w_plane_raw, t)
+
+        a_banks = [ps.tile([P, J], F32, name="a_bank%d" % t) for t in range(PACK)]
+        for t in range(PACK):
+            cols = slice(P * t, P * (t + 1))
+            nc.tensor.matmul_mx(
+                out=a_banks[t][:],
+                lhsT=w_dealt[:, cols].bitcast(E5M2),
+                lhsT_scale=w_plane[:, cols],
+                rhs=xg_words[:].bitcast(E4M3),
+                rhs_scale=xg_plane[:],
+                start=True,
+                stop=True,
+            )
+
+        wb_dealt = sb.tile([P, N], U16, name="wb_dealt", align_bytes=64)
+        wb_plane = sb.tile([P, N], U8, name="wb_plane", align_bytes=64)
+        deal(wb_dealt[:], wb_raw[:])
+
+        def on_vector(out, in_):
+            nc.vector.tensor_copy(out, in_)
+
+        def on_scalar(out, in_):
+            nc.scalar.activation(out, in_, COPY)
+
+        a_rows = [sb.tile([P, J], F32, name="a_rows%d" % t, align_bytes=64) for t in range(PACK)]
+        pick2 = sb.tile([P, PACK, O], F32, name="pick2", align_bytes=64)
+        pick3 = sb.tile([P, PACK, O], F32, name="pick3", align_bytes=64)
+
+        def look_up(move, t):
+            move(pick2[:, t, :], a_rows[t][:].indirect(list2[:]))
+            move(pick3[:, t, :], a_rows[t][:].indirect(list3[:]))
+
+        on_vector(a_rows[0][:], a_banks[0][:])
+        on_scalar(a_rows[1][:], a_banks[1][:])
+        on_scalar(a_rows[2][:], a_banks[2][:])
+        on_vector(a_rows[3][:], a_banks[3][:])
+        look_up(on_vector, 0)
+        look_up(on_scalar, 1)
+        look_up(on_scalar, 2)
+        look_up(on_vector, 3)
+
+        tz_pick = sb.tile([P, PACK, O], F32, name="tz_pick", align_bytes=64)
+        for t in range(PACK):
+            on_scalar(tz_pick[:, t, :], tz_rows[t][:].indirect(list4[:]))
+
+        def by_lines(rows):
+            return rows.rearrange("p t (c i) -> p c t i", i=PACK)
+
+        def woven(tile_ap):
+            return tile_ap.rearrange("p (c i) t -> p c t i", i=PACK)
+
+        hid = sb.tile([P, O, PACK], BF16, name="hid", align_bytes=64)
+        hid_words = sb.tile([P, O], U32, name="hid_words", align_bytes=64)
+        hid_plane = sb.tile([P, O], U8, name="hid_plane", align_bytes=64)
+        nc.vector.tensor_tensor(woven(hid[:]), by_lines(pick2[:]), by_lines(pick3[:]), MAX)
+        deal(wb_plane[:], wb_plane_raw[:])
+        nc.vector.quantize_mx(
+            out=hid_words[:].bitcast(E5M2), scales=hid_plane[:], in_=hid[:].rearrange("p o t -> p (o t)")
+        )
+
+        p_banks = [ps.tile([P, O], F32, name="p_bank%d" % t) for t in range(PACK)]
+        larger = sb.tile([P, PACK, O], F32, name="larger", align_bytes=64)
+        for t in range(PACK):
+            cols = slice(P * t, P * (t + 1))
+            nc.tensor.matmul_mx(
+                out=p_banks[t][:],
+                lhsT=wb_dealt[:, cols].bitcast(E2M1),
+                lhsT_scale=wb_plane[:, cols],
+                rhs=hid_words[:].bitcast(E5M2),
+                rhs_scale=hid_plane[:],
+                start=True,
+                stop=True,
+            )
+            nc.vector.tensor_tensor(larger[:, t, :], p_banks[t][:], tz_pick[:, t, :], MAX)
+
+        y = sb.tile([P, PACK, O], F32, name="y", align_bytes=64)
+        out_dealt = out_0.rearrange("(p t) o -> p t o", t=PACK)
+        y_bf = sb.tile([P, O, PACK], BF16, name="y_bf", align_bytes=64)
+        y_words = sb.tile([P, O], U32, name="y_words", align_bytes=64)
+        y_plane = sb.tile([P, O], U8, name="y_plane", align_bytes=64)
+
+        def weigh(pair):
+            nc.vector.tensor_tensor(
+                y[:, pair, :], larger[:, pair, :], rw_all[:].unsqueeze(1).to_broadcast([P, 2, O]), MULT
+            )
+            nc.sync.dma_start(out=out_dealt[:, pair, :], in_=y[:, pair, :])
+
+        weigh(slice(0, 2))
+        nc.vector.tensor_tensor(
+            woven(y_bf[:]), by_lines(larger[:]), by_lines(rw_all[:].unsqueeze(1).to_broadcast([P, PACK, O])), MULT
+        )
+        weigh(slice(2, 4))
+        nc.vector.quantize_mx(
+            out=y_words[:].bitcast(E4M3), scales=y_plane[:], in_=y_bf[:].rearrange("p o t -> p (o t)")
+        )
+        nc.scalar.dma_start(out=out_1[0].rearrange("p c t -> p (c t)").bitcast(I32), in_=y_words[:].bitcast(I32))
+        for q in range(QUADS):
+            queue = nc.scalar if q == QUADS - 1 else nc.sync
+            queue.dma_start(
+                out=out_2[0, PACK * q : PACK * (q + 1), :].bitcast(I32),
+                in_=y_plane[QUAD * q : QUAD * q + PACK, :].bitcast(I32),
+            )

@@ -1,6 +1,7 @@
 from contextlib import ExitStack
 
 import concourse.mybir as mybir
+from concourse.masks import make_identity
 
 K, T, J, R, O, N, Z = 512, 512, 256, 512, 128, 512, 512
 FLOPS = 2 * K * R * J + 2 * R * N * O
@@ -51,7 +52,9 @@ def tile_list_looks_picked_larger_floored_pl_kernel(
         wb_raw = sb.tile([P, N], U16, name="wb_raw", align_bytes=64)
         wb_plane_raw = sb.tile([P, N], U8, name="wb_plane_raw", align_bytes=64)
         tz_rows = [sb.tile([P, Z], F32, name="tz_rows%d" % t, align_bytes=64) for t in range(PACK)]
-        rw_all = sb.tile([P, O], F32, name="rw_all", align_bytes=64)
+        rw_column = sb.tile([P, 1], F32, name="rw_column", align_bytes=64)
+        identity = sb.tile([P, P], F32, name="identity", align_bytes=64)
+        make_identity(nc, identity[:])
 
         nc.sync.dma_start(list1[:], offs)
         load_scales_quadrant(nc.scalar, x_plane, xt_scales, 0)
@@ -69,15 +72,15 @@ def tile_list_looks_picked_larger_floored_pl_kernel(
         for q in range(QUADS):
             load_scales_quadrant(nc.sync, wb_plane_raw, wb_scales, q)
         nc.sync.dma_start(list4[:], offs4)
+        nc.sync.dma_start(out=rw_column[:], in_=rw.rearrange("one o -> o one"))
         tz_dealt = tz.rearrange("(p t) z -> p t z", t=PACK)
         for t in range(PACK):
             nc.sync.dma_start(out=tz_rows[t][:], in_=tz_dealt[:, t, :])
-        nc.sync.dma_start(out=rw_all[:], in_=rw[0].partition_broadcast(P))
 
         xg_words = sb.tile([P, J], U32, name="xg_words", align_bytes=64)
         xg_plane = sb.tile([P, J], U8, name="xg_plane", align_bytes=64)
-        nc.vector.tensor_copy(xg_words[:], x_words[:].indirect(list1[:]))
         nc.vector.tensor_copy(xg_plane[:], x_plane[:].indirect(list1[:]))
+        nc.vector.tensor_copy(xg_words[:], x_words[:].indirect(list1[:]))
 
         def deal(dealt, raw):
             nc.vector.tensor_copy(
@@ -94,7 +97,7 @@ def tile_list_looks_picked_larger_floored_pl_kernel(
         for t in range(PACK):
             deal_slot(w_plane, w_plane_raw, t)
 
-        a_banks = [ps.tile([P, J], F32, name="a_bank%d" % t) for t in range(PACK)]
+        a_banks = [ps.tile([P, J], F32, name="a_bank%d" % t, tag="bank%d" % t) for t in range(PACK)]
         for t in range(PACK):
             cols = slice(P * t, P * (t + 1))
             nc.tensor.matmul_mx(
@@ -144,6 +147,9 @@ def tile_list_looks_picked_larger_floored_pl_kernel(
         def woven(tile_ap):
             return tile_ap.rearrange("p (c i) t -> p c t i", i=PACK)
 
+        rw_all = ps.tile([P, O], F32, name="rw_all")
+        nc.tensor.transpose(rw_all[:], rw_column[:].to_broadcast([P, P]), identity[:])
+
         hid = sb.tile([P, O, PACK], BF16, name="hid", align_bytes=64)
         hid_words = sb.tile([P, O], U32, name="hid_words", align_bytes=64)
         hid_plane = sb.tile([P, O], U8, name="hid_plane", align_bytes=64)
@@ -153,7 +159,7 @@ def tile_list_looks_picked_larger_floored_pl_kernel(
             out=hid_words[:].bitcast(E5M2), scales=hid_plane[:], in_=hid[:].rearrange("p o t -> p (o t)")
         )
 
-        p_banks = [ps.tile([P, O], F32, name="p_bank%d" % t) for t in range(PACK)]
+        p_banks = [ps.tile([P, O], F32, name="p_bank%d" % t, tag="bank%d" % t) for t in range(PACK)]
         larger = sb.tile([P, PACK, O], F32, name="larger", align_bytes=64)
         for t in range(PACK):
             cols = slice(P * t, P * (t + 1))

@@ -51,7 +51,7 @@ def tile_list_looks_picked_larger_floored_pl_kernel(
         w_plane_raw = sb.tile([P, R], U8, name="w_plane_raw", align_bytes=64)
         wb_raw = sb.tile([P, N], U16, name="wb_raw", align_bytes=64)
         wb_plane_raw = sb.tile([P, N], U8, name="wb_plane_raw", align_bytes=64)
-        tz_rows = [sb.tile([P, Z], F32, name="tz_rows%d" % t, align_bytes=64) for t in range(PACK)]
+        tz_rows = [sb.tile([P, Z], F32, name="tz_rows%d" % t, tag="tz_rows%d" % t, align_bytes=64) for t in range(PACK)]
         rw_column = sb.tile([P, 1], F32, name="rw_column", align_bytes=64)
         identity = sb.tile([P, P], F32, name="identity", align_bytes=64)
         make_identity(nc, identity[:])
@@ -72,7 +72,7 @@ def tile_list_looks_picked_larger_floored_pl_kernel(
         for q in range(QUADS):
             load_scales_quadrant(nc.sync, wb_plane_raw, wb_scales, q)
         nc.sync.dma_start(list4[:], offs4)
-        nc.sync.dma_start(out=rw_column[:], in_=rw.rearrange("one o -> o one"))
+        nc.gpsimd.dma_start(out=rw_column[:], in_=rw.rearrange("one o -> o one"))
         tz_dealt = tz.rearrange("(p t) z -> p t z", t=PACK)
         for t in range(PACK):
             nc.sync.dma_start(out=tz_rows[t][:], in_=tz_dealt[:, t, :])
@@ -97,7 +97,7 @@ def tile_list_looks_picked_larger_floored_pl_kernel(
         for t in range(PACK):
             deal_slot(w_plane, w_plane_raw, t)
 
-        a_banks = [ps.tile([P, J], F32, name="a_bank%d" % t, tag="bank%d" % t) for t in range(PACK)]
+        a_banks = [ps.tile([P, J], F32, name="a_bank%d" % t, tag="a_bank%d" % t) for t in range(PACK)]
         for t in range(PACK):
             cols = slice(P * t, P * (t + 1))
             nc.tensor.matmul_mx(
@@ -147,8 +147,8 @@ def tile_list_looks_picked_larger_floored_pl_kernel(
         def woven(tile_ap):
             return tile_ap.rearrange("p (c i) t -> p c t i", i=PACK)
 
-        rw_all = ps.tile([P, O], F32, name="rw_all")
-        nc.tensor.transpose(rw_all[:], rw_column[:].to_broadcast([P, P]), identity[:])
+        rw_bank = ps.tile([P, O], F32, name="rw_bank", tag="a_bank3")
+        nc.tensor.transpose(rw_bank[:], rw_column[:].to_broadcast([P, P]), identity[:])
 
         hid = sb.tile([P, O, PACK], BF16, name="hid", align_bytes=64)
         hid_words = sb.tile([P, O], U32, name="hid_words", align_bytes=64)
@@ -159,7 +159,7 @@ def tile_list_looks_picked_larger_floored_pl_kernel(
             out=hid_words[:].bitcast(E5M2), scales=hid_plane[:], in_=hid[:].rearrange("p o t -> p (o t)")
         )
 
-        p_banks = [ps.tile([P, O], F32, name="p_bank%d" % t, tag="bank%d" % t) for t in range(PACK)]
+        p_banks = [ps.tile([P, O], F32, name="p_bank%d" % t) for t in range(PACK)]
         larger = sb.tile([P, PACK, O], F32, name="larger", align_bytes=64)
         for t in range(PACK):
             cols = slice(P * t, P * (t + 1))
@@ -174,23 +174,26 @@ def tile_list_looks_picked_larger_floored_pl_kernel(
             )
             nc.vector.tensor_tensor(larger[:, t, :], p_banks[t][:], tz_pick[:, t, :], MAX)
 
-        y = sb.tile([P, PACK, O], F32, name="y", align_bytes=64)
+        rw_all = sb.tile([P, O], F32, name="rw_all", tag="tz_rows3", align_bytes=64)
+        on_scalar(rw_all[:], rw_bank[:])
+        y_low = sb.tile([P, 2, O], F32, name="y_low", align_bytes=64)
+        y_high = sb.tile([P, 2, O], F32, name="y_high", align_bytes=64)
         out_dealt = out_0.rearrange("(p t) o -> p t o", t=PACK)
         y_bf = sb.tile([P, O, PACK], BF16, name="y_bf", align_bytes=64)
         y_words = sb.tile([P, O], U32, name="y_words", align_bytes=64)
         y_plane = sb.tile([P, O], U8, name="y_plane", align_bytes=64)
 
-        def weigh(pair):
+        def weigh(y_pair, pair):
             nc.vector.tensor_tensor(
-                y[:, pair, :], larger[:, pair, :], rw_all[:].unsqueeze(1).to_broadcast([P, 2, O]), MULT
+                y_pair[:], larger[:, pair, :], rw_all[:].unsqueeze(1).to_broadcast([P, 2, O]), MULT
             )
-            nc.sync.dma_start(out=out_dealt[:, pair, :], in_=y[:, pair, :])
+            nc.sync.dma_start(out=out_dealt[:, pair, :], in_=y_pair[:])
 
-        weigh(slice(0, 2))
+        weigh(y_low, slice(0, 2))
         nc.vector.tensor_tensor(
             woven(y_bf[:]), by_lines(larger[:]), by_lines(rw_all[:].unsqueeze(1).to_broadcast([P, PACK, O])), MULT
         )
-        weigh(slice(2, 4))
+        weigh(y_high, slice(2, 4))
         nc.vector.quantize_mx(
             out=y_words[:].bitcast(E4M3), scales=y_plane[:], in_=y_bf[:].rearrange("p o t -> p (o t)")
         )

from contextlib import ExitStack

import concourse.mybir as mybir
from concourse.masks import make_identity

K, T, J, R, O, N, Z = 512, 512, 256, 512, 128, 512, 512
FLOPS = 2 * K * R * J + 2 * R * N * O

F32 = mybir.dt.float32
BF16 = mybir.dt.bfloat16
I32 = mybir.dt.int32
U32 = mybir.dt.uint32
U16 = mybir.dt.uint16
U8 = mybir.dt.uint8
E4M3 = mybir.dt.float8_e4m3fn_x4
E5M2 = mybir.dt.float8_e5m2_x4
E2M1 = mybir.dt.float4_e2m1fn_x4
COPY = mybir.ActivationFunctionType.Copy
MAX = mybir.AluOpType.max
MULT = mybir.AluOpType.mult

P = 128
PACK = 4
QUADS = 4
QUAD = P // QUADS


def load_scales_quadrant(queue, plane, scales, q):
    rows = scales[0, PACK * q : PACK * (q + 1), :].bitcast(I32)
    queue.dma_start(
        out=plane[QUAD * q : QUAD * (q + 1), :].bitcast(I32),
        in_=rows.unsqueeze(0).to_broadcast([QUAD // PACK, PACK, rows.shape[1]]),
    )


def tile_list_looks_picked_larger_floored_pl_kernel(
    tc, xt_words, xt_scales, w_words, w_scales, wb_words, wb_scales, tz, rw, offs, offs2, offs3, offs4, out_0, out_1, out_2
):
    nc = tc.nc
    with ExitStack() as ctx:
        sb = ctx.enter_context(tc.tile_pool(name="sb", bufs=1))
        ps = ctx.enter_context(tc.psum_pool(name="ps", bufs=1))

        list1 = sb.tile([P, J // 16], U16, name="list1")
        list2 = sb.tile([P, O // 16], U16, name="list2")
        list3 = sb.tile([P, O // 16], U16, name="list3")
        list4 = sb.tile([P, O // 16], U16, name="list4")
        x_words = sb.tile([P, T], U32, name="x_words", align_bytes=64)
        x_plane = sb.tile([P, T], U8, name="x_plane", align_bytes=64)
        w_raw = sb.tile([P, R], U32, name="w_raw", align_bytes=64)
        w_plane_raw = sb.tile([P, R], U8, name="w_plane_raw", align_bytes=64)
        wb_raw = sb.tile([P, N], U16, name="wb_raw", align_bytes=64)
        wb_plane_raw = sb.tile([P, N], U8, name="wb_plane_raw", align_bytes=64)
        tz_rows = [sb.tile([P, Z], F32, name="tz_rows%d" % t, tag="tz_rows%d" % t, align_bytes=64) for t in range(PACK)]
        rw_column = sb.tile([P, 1], F32, name="rw_column", align_bytes=64)
        identity = sb.tile([P, P], F32, name="identity", align_bytes=64)
        make_identity(nc, identity[:])

        nc.sync.dma_start(list1[:], offs)
        load_scales_quadrant(nc.scalar, x_plane, xt_scales, 0)
        load_scales_quadrant(nc.sync, x_plane, xt_scales, 1)
        load_scales_quadrant(nc.scalar, x_plane, xt_scales, 2)
        load_scales_quadrant(nc.sync, x_plane, xt_scales, 3)
        nc.scalar.dma_start(out=x_words[:].bitcast(I32), in_=xt_words[0].rearrange("p c t -> p (c t)").bitcast(I32))
        load_scales_quadrant(nc.sync, w_plane_raw, w_scales, 0)
        nc.scalar.dma_start(out=w_raw[:].bitcast(I32), in_=w_words[0].rearrange("p c t -> p (c t)").bitcast(I32))
        for q in range(1, QUADS):
            load_scales_quadrant(nc.sync, w_plane_raw, w_scales, q)
        nc.sync.dma_start(list2[:], offs2)
        nc.sync.dma_start(list3[:], offs3)
        nc.sync.dma_start(out=wb_raw[:].bitcast(I32), in_=wb_words[0].bitcast(I32))
        for q in range(QUADS):
            load_scales_quadrant(nc.sync, wb_plane_raw, wb_scales, q)
        nc.sync.dma_start(list4[:], offs4)
        nc.gpsimd.dma_start(out=rw_column[:], in_=rw.rearrange("one o -> o one"))
        tz_dealt = tz.rearrange("(p t) z -> p t z", t=PACK)
        for t in range(PACK):
            nc.sync.dma_start(out=tz_rows[t][:], in_=tz_dealt[:, t, :])

        xg_words = sb.tile([P, J], U32, name="xg_words", align_bytes=64)
        xg_plane = sb.tile([P, J], U8, name="xg_plane", align_bytes=64)
        nc.vector.tensor_copy(xg_plane[:], x_plane[:].indirect(list1[:]))
        nc.vector.tensor_copy(xg_words[:], x_words[:].indirect(list1[:]))

        def deal(dealt, raw):
            nc.vector.tensor_copy(
                out=dealt.rearrange("p (t m) -> p m t", t=PACK), in_=raw.rearrange("p (m t) -> p m t", t=PACK)
            )

        w_dealt = sb.tile([P, R], U32, name="w_dealt", align_bytes=64)
        w_plane = sb.tile([P, R], U8, name="w_plane", align_bytes=64)
        deal(w_dealt[:].bitcast(I32), w_raw[:].bitcast(I32))

        def deal_slot(dealt, raw, t):
            nc.vector.tensor_copy(out=dealt[:, P * t : P * (t + 1)], in_=raw[:, t::PACK])

        for t in range(PACK):
            deal_slot(w_plane, w_plane_raw, t)

        a_banks = [ps.tile([P, J], F32, name="a_bank%d" % t, tag="a_bank%d" % t) for t in range(PACK)]
        for t in range(PACK):
            cols = slice(P * t, P * (t + 1))
            nc.tensor.matmul_mx(
                out=a_banks[t][:],
                lhsT=w_dealt[:, cols].bitcast(E5M2),
                lhsT_scale=w_plane[:, cols],
                rhs=xg_words[:].bitcast(E4M3),
                rhs_scale=xg_plane[:],
                start=True,
                stop=True,
            )

        wb_dealt = sb.tile([P, N], U16, name="wb_dealt", align_bytes=64)
        wb_plane = sb.tile([P, N], U8, name="wb_plane", align_bytes=64)
        deal(wb_dealt[:], wb_raw[:])

        def on_vector(out, in_):
            nc.vector.tensor_copy(out, in_)

        def on_scalar(out, in_):
            nc.scalar.activation(out, in_, COPY)

        a_rows = [sb.tile([P, J], F32, name="a_rows%d" % t, align_bytes=64) for t in range(PACK)]
        pick2 = sb.tile([P, PACK, O], F32, name="pick2", align_bytes=64)
        pick3 = sb.tile([P, PACK, O], F32, name="pick3", align_bytes=64)

        def look_up(move, t):
            move(pick2[:, t, :], a_rows[t][:].indirect(list2[:]))
            move(pick3[:, t, :], a_rows[t][:].indirect(list3[:]))

        on_vector(a_rows[0][:], a_banks[0][:])
        on_scalar(a_rows[1][:], a_banks[1][:])
        on_scalar(a_rows[2][:], a_banks[2][:])
        on_vector(a_rows[3][:], a_banks[3][:])
        look_up(on_vector, 0)
        look_up(on_scalar, 1)
        look_up(on_scalar, 2)
        look_up(on_vector, 3)

        tz_pick = sb.tile([P, PACK, O], F32, name="tz_pick", align_bytes=64)
        for t in range(PACK):
            on_scalar(tz_pick[:, t, :], tz_rows[t][:].indirect(list4[:]))

        def by_lines(rows):
            return rows.rearrange("p t (c i) -> p c t i", i=PACK)

        def woven(tile_ap):
            return tile_ap.rearrange("p (c i) t -> p c t i", i=PACK)

        rw_bank = ps.tile([P, O], F32, name="rw_bank", tag="a_bank3")
        nc.tensor.transpose(rw_bank[:], rw_column[:].to_broadcast([P, P]), identity[:])

        hid = sb.tile([P, O, PACK], BF16, name="hid", align_bytes=64)
        hid_words = sb.tile([P, O], U32, name="hid_words", align_bytes=64)
        hid_plane = sb.tile([P, O], U8, name="hid_plane", align_bytes=64)
        nc.vector.tensor_tensor(woven(hid[:]), by_lines(pick2[:]), by_lines(pick3[:]), MAX)
        deal(wb_plane[:], wb_plane_raw[:])
        nc.vector.quantize_mx(
            out=hid_words[:].bitcast(E5M2), scales=hid_plane[:], in_=hid[:].rearrange("p o t -> p (o t)")
        )

        p_banks = [ps.tile([P, O], F32, name="p_bank%d" % t) for t in range(PACK)]
        larger = sb.tile([P, PACK, O], F32, name="larger", align_bytes=64)
        for t in range(PACK):
            cols = slice(P * t, P * (t + 1))
            nc.tensor.matmul_mx(
                out=p_banks[t][:],
                lhsT=wb_dealt[:, cols].bitcast(E2M1),
                lhsT_scale=wb_plane[:, cols],
                rhs=hid_words[:].bitcast(E5M2),
                rhs_scale=hid_plane[:],
                start=True,
                stop=True,
            )
            nc.vector.tensor_tensor(larger[:, t, :], p_banks[t][:], tz_pick[:, t, :], MAX)

        rw_all = sb.tile([P, O], F32, name="rw_all", tag="tz_rows3", align_bytes=64)
        on_scalar(rw_all[:], rw_bank[:])
        y_low = sb.tile([P, 2, O], F32, name="y_low", align_bytes=64)
        y_high = sb.tile([P, 2, O], F32, name="y_high", align_bytes=64)
        out_dealt = out_0.rearrange("(p t) o -> p t o", t=PACK)
        y_bf = sb.tile([P, O, PACK], BF16, name="y_bf", align_bytes=64)
        y_words = sb.tile([P, O], U32, name="y_words", align_bytes=64)
        y_plane = sb.tile([P, O], U8, name="y_plane", align_bytes=64)

        def weigh(y_pair, pair):
            nc.vector.tensor_tensor(
                y_pair[:], larger[:, pair, :], rw_all[:].unsqueeze(1).to_broadcast([P, 2, O]), MULT
            )
            nc.sync.dma_start(out=out_dealt[:, pair, :], in_=y_pair[:])

        weigh(y_low, slice(0, 2))
        nc.vector.tensor_tensor(
            woven(y_bf[:]), by_lines(larger[:]), by_lines(rw_all[:].unsqueeze(1).to_broadcast([P, PACK, O])), MULT
        )
        weigh(y_high, slice(2, 4))
        nc.vector.quantize_mx(
            out=y_words[:].bitcast(E4M3), scales=y_plane[:], in_=y_bf[:].rearrange("p o t -> p (o t)")
        )
        nc.scalar.dma_start(out=out_1[0].rearrange("p c t -> p (c t)").bitcast(I32), in_=y_words[:].bitcast(I32))
        for q in range(QUADS):
            queue = nc.scalar if q == QUADS - 1 else nc.sync
            queue.dma_start(
                out=out_2[0, PACK * q : PACK * (q + 1), :].bitcast(I32),
                in_=y_plane[QUAD * q : QUAD * q + PACK, :].bitcast(I32),
            )
